import numpy as np
import ml_dtypes


def mxq(x, axis, fmt="e4m3"):
    dtype, down = {"e4m3": (ml_dtypes.float8_e4m3fn, 7), "e5m2": (ml_dtypes.float8_e5m2, 14)}[fmt]
    v = np.moveaxis(np.asarray(x, np.float32).astype(ml_dtypes.bfloat16).astype(np.float64), axis, -1)
    blocks = v.reshape(v.shape[:-1] + (-1, 32))
    amax = np.abs(blocks).max(-1, keepdims=True)
    byte = np.maximum(np.where(amax > 0, np.frexp(amax)[1] - 1 + 127, 0) - down, 1)
    scale = np.exp2(byte - 127.0)
    codes = (blocks / scale).astype(np.float32).astype(dtype).astype(np.float64)
    return np.moveaxis((codes * scale).reshape(v.shape), -1, axis)


WIDE = False


def mx_kscale(k):
    if not WIDE:
        return np.ones(k)
    levels = np.array([10, -10, 5, -5, 0])
    if k % 512:
        return np.exp2(np.random.permutation(np.resize(levels, k // 32))).repeat(32)
    a = np.empty((k // 512, 16))
    for p in range(k // 512):
        a[p, :8] = np.random.permutation(np.resize(levels, 8))
        for g in range(8):
            far = levels[np.abs(levels - a[p, g]) >= 10]
            a[p, g + 8] = far[np.random.randint(len(far))]
    return np.exp2(a.ravel()).repeat(32)


BF16 = ml_dtypes.bfloat16


def bf(x):
    return np.asarray(x, np.float32).astype(BF16)


def f64(x):
    return np.asarray(x).astype(np.float64)

def planes(Y):
    n, m = Y.shape
    b = f64(bf(Y)).reshape(n // 32, 32, m)
    amax = np.abs(b).max(1)
    byte = np.clip(np.where(amax > 0, np.frexp(amax)[1] - 1 + 127 - 7, 1), 1, 254)
    codes = (b * np.exp2(127.0 - byte)[:, None, :]).reshape(n, m).astype(np.float32).astype(ml_dtypes.float8_e4m3fn).view(np.uint8)
    words = codes.reshape(n // 512, 128, 4, m).transpose(0, 1, 3, 2)
    return np.ascontiguousarray(words), np.ascontiguousarray(byte.astype(np.uint8).reshape(n // 512, 16, m))


P, N, M = 1024, 1024, 1024
ETA = 0.5


def setup_inputs():
    s, c = mx_kscale(N), mx_kscale(M)
    return {"x": bf(np.random.standard_normal((P, N))),
            "g": bf((1.0 + 0.1 * np.random.standard_normal(N)) * s),
            "y": bf(np.random.standard_normal((P, M)) * c[None, :]),
            "a": bf(np.random.standard_normal((N, M)) / np.sqrt(N) / s[:, None] / c[None, :]),
            "b": bf(np.random.standard_normal((N, M)) / np.sqrt(N) / s[:, None] * c[None, :])}


def core(x, g, y, a, b):
    x, g, y, a, b = f64(x), f64(g), f64(y), f64(a), f64(b)
    t = np.tanh(x)
    u = g[None, :] * t
    uq = mxq(u, 1, "e4m3")
    ylook = y + ETA * (uq @ mxq(b, 0, "e4m3"))
    r = uq @ mxq(a, 0, "e4m3")
    direct = mxq(ylook, 1, "e4m3") @ mxq(a.T, 0, "e4m3")
    ahead = mxq(r, 1, "e4m3") @ mxq(b.T, 0, "e4m3")
    du = direct + ETA * ahead
    return (1.0 - t * t) * g[None, :] * du


def reference(x, g, y, a, b):
    R_out = core(x, g, y, a, b)
    words, scales = planes(R_out)
    return R_out, words, scales

from contextlib import ExitStack

import concourse.mybir as mybir
from concourse.masks import make_identity

F32 = mybir.dt.float32
BF16 = mybir.dt.bfloat16
U32 = mybir.dt.uint32
I32 = mybir.dt.int32
U8 = mybir.dt.uint8
FP8X4 = mybir.dt.float8_e4m3fn_x4
ACT = mybir.ActivationFunctionType
ALU = mybir.AluOpType

SIZE = 1024
P = 128
PACK = 4
GROUP = P * PACK
GROUPS = SIZE // GROUP
CHUNKS = GROUPS * PACK
BANKS = 8
ETA = 0.5
SLABS = {1: 2, 2: 3}
FLOPS = 4 * 2 * SIZE * SIZE * SIZE


def tile_lolabilinearlookaheadgradient_x1_kernel(tc, x, g, y, a, b, out_0, out_1, out_2):
    nc = tc.nc
    with ExitStack() as ctx:
        keep = ctx.enter_context(tc.tile_pool(name="keep", bufs=1))
        work = ctx.enter_context(tc.tile_pool(name="work", bufs=2))
        psum = ctx.enter_context(tc.psum_pool(name="psum", bufs=1))
        ctx.enter_context(tc.manual_schedule())

        tiles = {}
        banks_taken = []

        bank_of = {}
        busy = set()

        def new_bank(key):
            number = len(banks_taken) % BANKS
            banks_taken.append(number)
            busy.add(number)
            bank_of[key] = number
            tiles[key] = psum.tile([P, GROUP], F32, name="bank%d" % number)
            return tiles[key]

        def read_bank(key):
            busy.remove(bank_of[key])
            return tiles[key]

        def quantize(key, source, pool, tag, bufs):
            width = source.shape[1] // PACK
            codes = pool.tile([P, width], U32, name=tag + "_codes", bufs=bufs, align_bytes=64)
            scales = pool.tile([P, width], U8, name=tag + "_scales", bufs=bufs, align_bytes=64)
            nc.vector.quantize_mx(out=codes[:].bitcast(FP8X4), scales=scales[:], in_=source)
            tiles[key] = (codes, scales)

        def mx_pass(out, still, still_cols, moving, moving_cols, start, stop):
            nc.tensor.matmul_mx(
                out=out,
                lhsT=still[0][:, still_cols].bitcast(FP8X4),
                lhsT_scale=still[1][:, still_cols],
                rhs=moving[0][:, moving_cols].bitcast(FP8X4),
                rhs_scale=moving[1][:, moving_cols],
                start=start,
                stop=stop,
            )

        def block(i):
            return slice(i * P, (i + 1) * P)

        def group_rows(matrix, grp):
            return matrix[grp * GROUP : (grp + 1) * GROUP, :].rearrange("(p t) n -> p t n", t=PACK)

        def load_matrix(which, grp, halves):
            width = len(halves) * GROUP
            slab = work.tile([P, PACK, width], BF16, name="slab%d" % len(halves), bufs=SLABS[len(halves)], align_bytes=64)
            cols = slice(halves[0] * GROUP, halves[0] * GROUP + width)
            nc.sync.dma_start(out=slab[:], in_=group_rows({"a": a, "b": b}[which], grp)[:, :, cols])
            for i, half in enumerate(halves):
                tiles["raw", (which, grp, half)] = slab[:, :, i * GROUP : (i + 1) * GROUP]

        def load_gain_rows():
            nc.sync.dma_start(out=g_rows[:], in_=g.partition_broadcast(P))
            tiles["g_rows"] = g_rows

        def load_rows(which, c):
            rows = work.tile([P, SIZE], BF16, name=which + "_rows", bufs=4, align_bytes=64)
            nc.sync.dma_start(out=rows[:], in_=group_rows({"x": x, "y": y}[which], c // PACK)[:, c % PACK, :])
            tiles[which, c] = rows

        def interleave(piece, engine):
            which = piece[0]
            raw = tiles["raw", piece]
            grouped = work.tile([P, GROUP * PACK], BF16, name="grouped_" + engine, bufs=2, align_bytes=64)
            if which == "b":
                src = raw.rearrange("p j (c i) -> p c j i", i=4)
                dst = grouped[:].rearrange("p (c i j) -> p c j i", i=4, j=PACK)
                if engine == "vector":
                    nc.vector.tensor_scalar(out=dst, in0=src, scalar1=ETA, scalar2=None, op0=ALU.mult)
                else:
                    nc.scalar.activation(out=dst, in_=src, func=ACT.Copy, scale=ETA)
            else:
                src = raw.rearrange("p j (m t) -> p m j t", t=PACK)
                dst = grouped[:].rearrange("p (t m j) -> p m j t", t=PACK, j=PACK)
                if engine == "vector":
                    nc.vector.tensor_copy(out=dst, in_=src)
                else:
                    nc.scalar.copy(out=dst, in_=src)
            tiles["grouped0", piece] = grouped

        def quantize_axis0(piece):
            quantize(("q0", piece), tiles["grouped0", piece][:], keep, "q0_%s%d%d" % piece, 1)

        def turn_piece(piece):
            raw = tiles["raw", piece]
            for pair in range(2):
                bank = new_bank(("turned", piece, pair))
                for jj in range(2):
                    words = raw[:, 2 * pair + jj, :].bitcast(F32)
                    for u in range(2):
                        nc.tensor.transpose(bank[:, block(2 * jj + u)], words[:, u : 2 * P : 2], ident[:])

        def empty_piece(piece):
            grouped = work.tile([P, GROUP * PACK], BF16, name="grouped1", bufs=6, align_bytes=64)
            words = grouped[:].bitcast(F32).rearrange("q (p k) -> q p k", k=8)
            for pair in range(2):
                nc.scalar.copy(
                    out=words[:, :, 4 * pair : 4 * pair + 4],
                    in_=read_bank(("turned", piece, pair))[:].rearrange("q (k p) -> q p k", k=4),
                )
            tiles["grouped1", piece] = grouped

        def quantize_axis1(piece):
            quantize(("q1", piece), tiles["grouped1", piece][:], keep, "q1_%s%d%d" % piece, 1)

        def tanh(c):
            th = work.tile([P, SIZE], F32, name="tanh", bufs=CHUNKS)
            nc.scalar.activation(
                out=th[:].rearrange("p (t q) -> p t q", t=PACK),
                in_=tiles["x", c][:].rearrange("p (q t) -> p t q", t=PACK),
                func=ACT.Tanh,
            )
            tiles["tanh", c] = th

        def turn_tanh(c):
            th = tiles["tanh", c]
            for grp in range(GROUPS):
                bank = new_bank(("tanh_T", c, grp))
                for t in range(PACK):
                    nc.tensor.transpose(bank[:, block(t)], th[:, block(GROUPS * t + grp)], ident[:])

        def make_u(c, grp):
            if grp == 0:
                tiles["u", c] = work.tile([P, GROUPS, GROUP], BF16, name="u", align_bytes=64)
            nc.vector.tensor_tensor(
                out=tiles["u", c][:, grp, :].rearrange("p (r t) -> p r t", t=PACK),
                in0=read_bank(("tanh_T", c, grp))[:].rearrange("p (t r) -> p r t", t=PACK),
                in1=g_cols[:, grp, :].unsqueeze(1).to_broadcast([P, P, PACK]),
                op=ALU.mult,
            )
            tiles["u", c, grp] = True

        def quantize_u(c):
            quantize(("uq", c), tiles["u", c][:].rearrange("p g n -> p (g n)"), work, "uq", 4)

        def mx_ylook(c):
            for half in range(GROUPS):
                bank = new_bank(("ylook_sum", c, half))
                for grp in range(GROUPS):
                    mx_pass(bank[:], tiles["uq", c], block(grp), tiles["q0", ("b", grp, half)], slice(0, GROUP),
                            grp == 0, grp == GROUPS - 1)

        def mx_r(c):
            for half in range(GROUPS):
                bank = new_bank(("r_sum", c, half))
                for t in range(PACK):
                    for grp in range(GROUPS):
                        mx_pass(bank[:, block(t)], tiles["q0", ("a", grp, half)], block(t), tiles["uq", c], block(grp),
                                grp == 0, grp == GROUPS - 1)

        def add_y(c, half):
            if half == 0:
                tiles["ylook", c] = work.tile([P, GROUPS, GROUP], BF16, name="ylook", align_bytes=64)
            nc.vector.tensor_tensor(
                out=tiles["ylook", c][:, half, :].rearrange("r (u p e) -> r u p e", u=2, e=2),
                in0=read_bank(("ylook_sum", c, half))[:].rearrange("r (p u e) -> r u p e", u=2, e=2),
                in1=tiles["y", c][:, half * GROUP : (half + 1) * GROUP].rearrange("r (p u e) -> r u p e", u=2, e=2),
                op=ALU.add,
            )
            tiles["ylook", c, half] = True

        def turn_ylook(c):
            bank = new_bank(("ylook_T", c))
            words = tiles["ylook", c][:].rearrange("r h n -> r (h n)").bitcast(F32)
            for i in range(4):
                nc.tensor.transpose(bank[:, block(i)], words[:, block(i)], ident[:])

        def second(c):
            if ("second", c) not in tiles:
                tiles["second", c] = work.tile([P, 4, GROUP], BF16, name="second", bufs=3, align_bytes=64)
            return tiles["second", c]

        def empty_ylook(c):
            words = second(c)[:, 0:2, :].rearrange("p h n -> p (h n)").bitcast(F32)
            nc.scalar.copy(
                out=words.rearrange("p (h r u) -> p h r u", h=2, u=2),
                in_=read_bank(("ylook_T", c))[:].rearrange("p (h u r) -> p h r u", h=2, u=2),
            )
            tiles["second", c, "ylook"] = True

        def empty_r(c, half):
            nc.scalar.activation(
                out=second(c)[:, 2 + half, :].rearrange("p (r t) -> p r t", t=PACK),
                in_=read_bank(("r_sum", c, half))[:].rearrange("p (t r) -> p r t", t=PACK),
                func=ACT.Copy,
                scale=ETA,
            )
            tiles["second", c, half] = True

        def quantize_second(c):
            quantize(("sq2", c), second(c)[:].rearrange("p h n -> p (h n)"), keep, "second%d" % c, 1)

        def square(part):
            grp, first, width = part
            w = work.tile([P, PACK, width], F32, name="factor", bufs=3)
            for row in range(PACK):
                th = tiles["tanh", PACK * grp + row][:].rearrange("p (t q) -> p t q", t=PACK)
                nc.scalar.activation(
                    out=w[:, row, :].rearrange("p (k i t) -> p k t i", i=4, t=PACK),
                    in_=th[:, :, first // PACK : (first + width) // PACK].rearrange("p t (k i) -> p k t i", i=4),
                    func=ACT.Square,
                )
            tiles["square", part] = w

        def factor(part):
            grp, first, width = part
            w = tiles["square", part]
            nc.vector.scalar_tensor_tensor(
                out=w[:], in0=w[:], scalar=1.0,
                in1=g_rows[:, first : first + width].unsqueeze(1).to_broadcast([P, PACK, width]),
                op0=ALU.subtract, op1=ALU.mult,
            )
            tiles["factor", part] = w

        def mx_out(part):
            grp, first, width = part
            half, start = divmod(first, GROUP)
            per_bank = GROUP // width
            for t in range(PACK):
                if t % per_bank == 0:
                    bank = new_bank(("du", part, t // per_bank))
                place = (t % per_bank) * width
                partners = [("a", half, 0), ("a", half, 1), ("b", half, 0), ("b", half, 1)]
                for i, piece in enumerate(partners):
                    mx_pass(bank[:, place : place + width], tiles["sq2", PACK * grp + t], block(i),
                            tiles["q1", piece], slice(start, start + width), i == 0, i == len(partners) - 1)

        def finish(part, i):
            grp, first, width = part
            per_bank = GROUP // width
            if i == 0:
                tiles["res", part] = work.tile([P, PACK, width], F32, name="slab2", bufs=SLABS[2], align_bytes=64)
            rows = slice(i * per_bank, (i + 1) * per_bank)
            nc.vector.scalar_tensor_tensor(
                out=tiles["res", part][:, rows, :],
                in0=read_bank(("du", part, i))[:].rearrange("p (t n) -> p t n", t=per_bank),
                scalar=-1.0,
                in1=tiles["factor", part][:, rows, :],
                op0=ALU.mult, op1=ALU.mult,
            )
            tiles["res", part, i] = True

        def store_result(part):
            grp, first, width = part
            nc.sync.dma_start(out=group_rows(out_0, grp)[:, :, first : first + width], in_=tiles["res", part][:])

        def round_result(part, engine, lo, hi):
            grp, first, width = part
            if lo == 0:
                tiles["resbf", part] = work.tile([P, width * PACK], BF16, name="grouped_scalar", bufs=2, align_bytes=64)
            src = tiles["res", part][:, :, lo:hi].rearrange("p t (c i) -> p c t i", i=4)
            dst = tiles["resbf", part][:, lo * PACK : hi * PACK].rearrange("p (c i t) -> p c t i", i=4, t=PACK)
            if engine == "vector":
                nc.vector.tensor_copy(out=dst, in_=src)
            else:
                nc.scalar.copy(out=dst, in_=src)
            tiles["resbf", part, hi] = True

        def quantize_result(part):
            grp, first, width = part
            cols = slice(first, first + width)
            nc.vector.quantize_mx(out=out_codes[grp][:, cols].bitcast(FP8X4), scales=out_scales[grp][:, cols],
                                  in_=tiles["resbf", part][:])
            tiles["planes", part] = True

        def store_words(part):
            grp, first, width = part
            cols = slice(first, first + width)
            nc.sync.dma_start(out=out_1[grp, :, cols, :].rearrange("p m t -> p (m t)").bitcast(I32),
                              in_=out_codes[grp][:, cols].bitcast(I32))

        def store_scales(grp, engine, quads, last):
            for quad in quads:
                {"sync": nc.sync, "scalar": nc.scalar}[engine].dma_start(
                    out=out_2[grp, 4 * quad : 4 * quad + 4, :].bitcast(I32),
                    in_=out_scales[grp][32 * quad : 32 * quad + 4, :].bitcast(I32))

        ident = keep.tile([P, P], F32, name="ident")
        g_cols = keep.tile([P, GROUPS, PACK], BF16, name="g_cols")
        g_rows = keep.tile([P, SIZE], BF16, name="g_bc")
        warm = keep.tile([P, 2], F32, name="warm")
        out_codes = [keep.tile([P, SIZE], U32, name="out_codes%d" % i, align_bytes=64) for i in range(GROUPS)]
        out_scales = [keep.tile([P, SIZE], U8, name="out_scales%d" % i, align_bytes=64) for i in range(GROUPS)]

        def halves_of(key, c):
            return [(key, c, half) for half in range(GROUPS)]

        def pieces_of(key, matrices):
            return [(key, (which, grp, half)) for which in matrices for grp in range(GROUPS) for half in range(GROUPS)]

        def all_results(part):
            return [("res", part, i) for i in range(part[2] // P)]

        needs = {
            interleave: lambda piece, engine: [("raw", piece)],
            quantize_axis0: lambda piece: [("grouped0", piece)],
            turn_piece: lambda piece: [("raw", piece)],
            empty_piece: lambda piece: [("turned", piece, 1)],
            quantize_axis1: lambda piece: [("grouped1", piece)],
            tanh: lambda c: [("x", c)],
            turn_tanh: lambda c: [("tanh", c)],
            make_u: lambda c, grp: [("tanh_T", c, grp)],
            quantize_u: lambda c: halves_of("u", c),
            mx_ylook: lambda c: [("uq", c)] + pieces_of("q0", "b"),
            mx_r: lambda c: [("uq", c)] + pieces_of("q0", "a"),
            add_y: lambda c, half: [("ylook_sum", c, half), ("y", c)],
            turn_ylook: lambda c: halves_of("ylook", c),
            empty_ylook: lambda c: [("ylook_T", c)],
            empty_r: lambda c, half: [("r_sum", c, half)],
            quantize_second: lambda c: halves_of("second", c) + [("second", c, "ylook")],
            square: lambda part: [("tanh", PACK * part[0] + row) for row in range(PACK)],
            factor: lambda part: [("square", part), "g_rows"],
            mx_out: lambda part: [("sq2", PACK * part[0] + row) for row in range(PACK)] + pieces_of("q1", "ab"),
            finish: lambda part, i: [("du", part, i), ("factor", part)],
            store_result: all_results,
            round_result: lambda part, engine, lo, hi: all_results(part) + ([("resbf", part, lo)] if lo else []),
            quantize_result: lambda part: [("resbf", part, part[2])],
            store_words: lambda part: [("planes", part)],
            store_scales: lambda grp, engine, quads, last: [("planes", last)],
            load_rows: lambda which, c: [{"x": ("tanh", c - 4), "y": ("ylook", c - 4, 1)}[which]] if c >= 4 else [],
        }
        banks_wanted = {turn_piece: lambda piece: 2, turn_tanh: lambda c: 2, mx_ylook: lambda c: 2, mx_r: lambda c: 2,
                        turn_ylook: lambda c: 1, mx_out: lambda part: part[2] // P}

        def ready(step):
            work_fn, args = step[0], step[1:]
            if work_fn in banks_wanted:
                for i in range(banks_wanted[work_fn](*args)):
                    if (len(banks_taken) + i) % BANKS in busy:
                        return False
            return work_fn not in needs or all(key in tiles for key in needs[work_fn](*args))

        nc.scalar.dma_start(out=g_cols[:], in_=g.rearrange("(g p t) -> p g t", p=P, t=PACK))
        make_identity(nc, ident[:])
        nc.vector.memset(warm[:, 0:1], 0.0)
        nc.scalar.activation(out=warm[:, 1:2], in_=warm[:, 0:1], func=ACT.Tanh)


        b00, b01, b10, b11 = [("b", grp, half) for grp in range(2) for half in range(2)]
        a00, a01, a10, a11 = [("a", grp, half) for grp in range(2) for half in range(2)]
        parts = [(0, i * 256, 256) for i in range(4)] + [(1, i * 256, 256) for i in range(3)] + [(1, 768, 128), (1, 896, 128)]

        sync_q = [(load_matrix, "b", 0, [0]), (load_rows, "x", 0), (load_matrix, "b", 0, [1]), (load_matrix, "b", 1, [0, 1]),
                  (load_rows, "x", 1), (load_matrix, "a", 0, [0, 1]), (load_rows, "y", 0), (load_matrix, "a", 1, [0, 1]),
                  (load_rows, "x", 2), (load_rows, "y", 1), (load_rows, "x", 3), (load_rows, "y", 2), (load_rows, "y", 3)]
        sync_q += [(load_rows, "x", 4), (load_rows, "x", 5), (load_gain_rows,)]
        sync_q += [(load_rows, "y", 4), (load_rows, "x", 6), (load_rows, "y", 5), (load_rows, "x", 7), (load_rows, "y", 6), (load_rows, "y", 7)]
        for k, part in enumerate(parts):
            sync_q += [(store_result, part)]
            if k > 0:
                sync_q += [(store_words, parts[k - 1])]
            if k == 4:
                sync_q += [(store_scales, 0, "sync", range(4), parts[3])]
        sync_q += [(store_words, parts[-1]), (store_scales, 1, "sync", range(2), parts[-1])]

        tensor_q = [(turn_piece, b00), (turn_tanh, 0), (turn_piece, b01), (turn_piece, b10), (turn_piece, b11), (turn_tanh, 1),
                    (turn_piece, a00), (turn_piece, a01), (mx_ylook, 0), (turn_piece, a10), (turn_piece, a11)]
        scalar_q = [(tanh, 0), (empty_piece, b00), (empty_piece, b01), (tanh, 1), (empty_piece, b10), (empty_piece, b11),
                    (interleave, a01, "scalar"), (empty_piece, a00), (tanh, 2), (empty_piece, a01), (interleave, a11, "scalar"),
                    (empty_piece, a10), (empty_piece, a11)]
        vector_q = [(interleave, b00, "vector"), (quantize_axis0, b00), (interleave, b01, "vector"), (make_u, 0, 0), (make_u, 0, 1),
                    (quantize_axis0, b01), (interleave, b10, "vector"), (quantize_u, 0), (interleave, b11, "vector"),
                    (quantize_axis0, b10), (quantize_axis1, b00), (quantize_axis0, b11),
                    (make_u, 1, 0), (make_u, 1, 1), (interleave, a00, "vector"), (quantize_u, 1), (quantize_axis1, b01),
                    (add_y, 0, 0), (add_y, 0, 1), (interleave, a10, "vector"), (quantize_axis0, a00), (quantize_axis0, a01),
                    (quantize_axis1, b10), (quantize_axis0, a10), (quantize_axis1, b11), (quantize_axis0, a11)]
        fill = {1: [a00], 2: [a01, a10], 3: [a11]}
        part_at = {5 + k: k for k in range(len(parts))}
        for s in range(1, 17):
            def chunk(c):
                return 0 <= c < CHUNKS
            now = parts[part_at[s]] if s in part_at else None
            nxt = parts[part_at[s + 1]] if s + 1 in part_at else None
            done = parts[part_at[s - 1]] if s - 1 in part_at else None
            old = parts[part_at[s - 2]] if s - 2 in part_at else None
            if chunk(s - 1):
                tensor_q += [(turn_ylook, s - 1)]
            if chunk(s + 1):
                tensor_q += [(turn_tanh, s + 1)]
            if chunk(s):
                tensor_q += [(mx_ylook, s)]
            if chunk(s - 1):
                tensor_q += [(mx_r, s - 1)]
            if now:
                tensor_q += [(mx_out, now)]

            if chunk(s - 1):
                scalar_q += [(empty_ylook, s - 1)]
            if chunk(s + 2):
                scalar_q += [(tanh, s + 2)]
            if done:
                scalar_q += [(round_result, done, "scalar", 0, done[2])]
            if s + 2 in part_at:
                scalar_q += [(square, parts[part_at[s + 2]])]
            if chunk(s - 1):
                scalar_q += [(empty_r, s - 1, 0), (empty_r, s - 1, 1)]

            if done:
                vector_q += [(finish, done, i) for i in range(done[2] // P)]
            if chunk(s - 2):
                vector_q += [(quantize_second, s - 2)]
            if old:
                vector_q += [(quantize_result, old)]
            if chunk(s + 1):
                vector_q += [(make_u, s + 1, 0), (make_u, s + 1, 1)]
            if chunk(s):
                vector_q += [(add_y, s, 0), (add_y, s, 1)]
            if chunk(s + 1):
                vector_q += [(quantize_u, s + 1)]
            vector_q += [(quantize_axis1, piece) for piece in fill.get(s, [])]
            if nxt:
                vector_q += [(factor, nxt)]
        scalar_q += [(store_scales, 1, "scalar", range(2, 4), parts[-1])]

        queues = [sync_q, tensor_q, scalar_q, vector_q]
        places = [0] * len(queues)
        while any(places[i] < len(queue) for i, queue in enumerate(queues)):
            before = sum(places)
            for i, queue in enumerate(queues):
                if places[i] < len(queue) and ready(queue[places[i]]):
                    step = queue[places[i]]
                    step[0](*step[1:])
                    places[i] += 1
            assert sum(places) > before, [queue[places[i]] for i, queue in enumerate(queues) if places[i] < len(queue)]
